import numpy as np
import ml_dtypes


def mxq(x, axis, fmt="e4m3"):
    dtype, down = {"e4m3": (ml_dtypes.float8_e4m3fn, 7), "e5m2": (ml_dtypes.float8_e5m2, 14)}[fmt]
    v = np.moveaxis(np.asarray(x, np.float32).astype(ml_dtypes.bfloat16).astype(np.float64), axis, -1)
    blocks = v.reshape(v.shape[:-1] + (-1, 32))
    amax = np.abs(blocks).max(-1, keepdims=True)
    byte = np.maximum(np.where(amax > 0, np.frexp(amax)[1] - 1 + 127, 0) - down, 1)
    scale = np.exp2(byte - 127.0)
    codes = (blocks / scale).astype(np.float32).astype(dtype).astype(np.float64)
    return np.moveaxis((codes * scale).reshape(v.shape), -1, axis)


WIDE = False


def mx_kscale(k):
    if not WIDE:
        return np.ones(k)
    levels = np.array([10, -10, 5, -5, 0])
    if k % 512:
        return np.exp2(np.random.permutation(np.resize(levels, k // 32))).repeat(32)
    a = np.empty((k // 512, 16))
    for p in range(k // 512):
        a[p, :8] = np.random.permutation(np.resize(levels, 8))
        for g in range(8):
            far = levels[np.abs(levels - a[p, g]) >= 10]
            a[p, g + 8] = far[np.random.randint(len(far))]
    return np.exp2(a.ravel()).repeat(32)


def f64(x):
    return np.asarray(x).astype(np.float64)


def striped(idx):
    return np.tile(idx.reshape(-1, 16).T, (8, 1)).astype(np.uint16)


def unstriped(offs):
    return offs[:16].T.reshape(-1).astype(np.int64)


E2M1 = np.array([0.0, 0.5, 1.0, 1.5, 2.0, 3.0, 4.0, 6.0, -0.0, -0.5, -1.0, -1.5, -2.0, -3.0, -4.0, -6.0])


def pack_weight(w, fmt):
    k, n = w.shape
    w = f64(np.asarray(w, np.float32).astype(ml_dtypes.bfloat16)).reshape(k // 32, 32, n)
    amax = np.abs(w).max(1)
    if fmt == "e4m3":
        byte = np.frexp(amax)[1] - 1 + 127 - 7
    else:
        mant, ex = np.frexp(amax / 6.0)
        byte = np.where(mant > 0.5, ex, ex - 1) + 127
    byte = np.clip(np.where(amax > 0, byte, 1), 1, 254)
    scaled = (w * np.exp2(127.0 - byte)[:, None, :]).reshape(k, n).astype(np.float32)
    by_word = np.ascontiguousarray(scaled.reshape(k // 512, 128, 4, n).transpose(0, 1, 3, 2))
    if fmt == "e4m3":
        words = by_word.astype(ml_dtypes.float8_e4m3fn).view(np.uint8)
    else:
        c = by_word.astype(ml_dtypes.float4_e2m1fn).view(np.uint8) & 0xF
        words = (c[..., 0::2] | (c[..., 1::2] << 4)).reshape(k // 512, 128, 2 * n)
    return np.ascontiguousarray(words), np.ascontiguousarray(byte.astype(np.uint8).reshape(k // 512, 16, n))


def unpack_weight(words, scales, fmt):
    g, _, n = scales.shape
    words = np.ascontiguousarray(words).reshape(g, 128, n, -1)
    if fmt == "e4m3":
        vals = words.view(ml_dtypes.float8_e4m3fn).astype(np.float64)
    else:
        nib = np.empty((g, 128, n, 4), np.uint8)
        nib[..., 0::2] = words & 0xF
        nib[..., 1::2] = words >> 4
        vals = E2M1[nib]
    vals = vals * np.repeat(np.exp2(scales.astype(np.float64) - 127.0), 8, axis=1)[..., None]
    return vals.transpose(0, 1, 3, 2).reshape(g * 512, n)


def pack_table(v):
    words, scales = pack_weight(v, "e4m3")
    return np.concatenate([words.reshape(words.shape[0], -1), scales.reshape(scales.shape[0], -1)], axis=1)


def unpack_table(tab):
    g, t = tab.shape[0], tab.shape[1] // 528
    return unpack_weight(tab[:, :512 * t].reshape(g, 128, t, 4), tab[:, 512 * t:].reshape(g, 16, t), "e4m3")


K, M, T, S = 1024, 1024, 4096, 1536


def setup_inputs():
    n = np.random.standard_normal
    s = mx_kscale(K)[:, None]
    return {
        "tab": pack_table(n((K, T)) * s),
        "w": (n((K, M)) / np.sqrt(K) / s).astype(np.float32),
        "offs": striped(np.random.permutation(T)[:S]),
    }


def reference(tab, w, offs):
    tab_ = unpack_table(tab)[:, unstriped(offs)]
    w_ = mxq(f64(w), 0, "e4m3")
    y = tab_.T @ w_
    return y

@@ -1,0 +1,157 @@
+from contextlib import ExitStack
+
+import concourse.mybir as mybir
+
+K, N, T, S = 1024, 1024, 4096, 1536
+
+FLOPS = 2 * K * N * S
+BYTES = 2 * 528 * T + 4 * K * N + 2 * 128 * (S // 16) + 4 * S * N
+
+F32 = mybir.dt.float32
+BF16 = mybir.dt.bfloat16
+I32 = mybir.dt.int32
+U32 = mybir.dt.uint32
+U16 = mybir.dt.uint16
+U8 = mybir.dt.uint8
+FP8X4 = mybir.dt.float8_e4m3fn_x4
+
+P = 128
+PACK = 4
+K_PASS = P * PACK
+PASSES = K // K_PASS
+J_TILE = 128
+N_HALF = 512
+J_TILES = S // J_TILE
+SCALE_ROWS = 4
+BANKS = 8
+AHEAD = 4
+EARLY = 6
+
+
+def tile_list_tabw_tm_none_kernel(tc, tab, w, offs, out):
+    nc = tc.nc
+
+    with ExitStack() as ctx:
+        held = ctx.enter_context(tc.tile_pool(name="held", bufs=1))
+        psum = ctx.enter_context(tc.psum_pool(name="psum", bufs=BANKS))
+
+        offsets = held.tile([P, S // 16], U16, name="offsets")
+        words = [held.tile([P, T], I32, name=f"words{a}", align_bytes=64) for a in range(PASSES)]
+        scale_rows = held.tile([P, T // 4], I32, name="scale_rows", align_bytes=64)
+        picked = [held.tile([P, S], U32, name=f"picked{a}", align_bytes=64) for a in range(PASSES)]
+        picked_scales = held.tile([P, S], U8, name="picked_scales", align_bytes=64)
+        raw0 = held.tile([P, PACK, N], F32, name="raw0")
+        raw1 = [held.tile([P, PACK, N_HALF], F32, name=f"raw1_{h}") for h in range(2)]
+        grouped = [
+            [held.tile([P, N_HALF, PACK], BF16, name=f"grouped{a}_{h}", align_bytes=64) for h in range(2)]
+            for a in range(PASSES)
+        ]
+        w_codes = [
+            [held.tile([P, N_HALF], U32, name=f"w_codes{a}_{h}", align_bytes=64) for h in range(2)]
+            for a in range(PASSES)
+        ]
+        w_scales = [
+            [held.tile([P, N_HALF], U8, name=f"w_scales{a}_{h}", align_bytes=64) for h in range(2)]
+            for a in range(PASSES)
+        ]
+        results = [held.tile([P, N], F32, name=f"result{j}") for j in range(J_TILES)]
+
+        tab_words = tab.bitcast(I32)
+        row_words = T // 4
+
+        nc.sync.dma_start(offsets[:], offs)
+        nc.sync.dma_start(out=words[0][:], in_=tab_words[0, 0 : P * T].rearrange("(p t) -> p t", t=T))
+        nc.vector.memset(scale_rows[:], 0)
+        for q in range(4):
+            nc.scalar.dma_start(
+                out=scale_rows[32 * q : 32 * q + PASSES * SCALE_ROWS, :],
+                in_=tab_words[:, P * T : P * T + 16 * row_words].rearrange("a (r t) -> a r t", t=row_words)[
+                    :, SCALE_ROWS * q : SCALE_ROWS * (q + 1), :
+                ],
+            )
+        nc.sync.dma_start(out=words[1][:], in_=tab_words[1, 0 : P * T].rearrange("(p t) -> p t", t=T))
+        nc.sync.dma_start(out=raw0[:], in_=w[0:K_PASS, :].rearrange("(p i) n -> p i n", i=PACK))
+        for h in range(2):
+            nc.sync.dma_start(
+                out=raw1[h][:],
+                in_=w[K_PASS:K, N_HALF * h : N_HALF * (h + 1)].rearrange("(p i) n -> p i n", i=PACK),
+            )
+
+        nc.vector.tensor_copy(picked_scales[:], scale_rows[:].bitcast(U8).indirect(offsets[:]))
+        for a in range(PASSES):
+            nc.vector.tensor_copy(picked[a][:], words[a][:].bitcast(U32).indirect(offsets[:]))
+
+        def interleave(copy, a, h, c0, c1):
+            src = raw0[:, :, N_HALF * h + c0 : N_HALF * h + c1] if a == 0 else raw1[h][:, :, c0:c1]
+            copy(
+                out=grouped[a][h][:, c0:c1, :].rearrange("p (c i) t -> p c t i", i=4),
+                in_=src.rearrange("p t (c i) -> p c t i", i=4),
+            )
+
+        def quantize(a, h, c0, c1):
+            nc.vector.quantize_mx(
+                out=w_codes[a][h][:, c0:c1].bitcast(FP8X4),
+                scales=w_scales[a][h][:, c0:c1],
+                in_=grouped[a][h][:, c0:c1, :].rearrange("p c t -> p (c t)"),
+            )
+
+        vector, scalar = nc.vector.tensor_copy, nc.scalar.copy
+        interleave(vector, 0, 0, 0, 256)
+        interleave(vector, 0, 0, 256, 512)
+        interleave(scalar, 0, 1, 0, 256)
+        interleave(scalar, 0, 1, 256, 512)
+        quantize(0, 0, 0, 256)
+        quantize(0, 0, 256, 512)
+        interleave(scalar, 1, 0, 384, 512)
+        interleave(vector, 1, 0, 0, 256)
+        interleave(vector, 1, 0, 256, 384)
+        quantize(1, 0, 0, 256)
+        quantize(1, 0, 256, 384)
+        quantize(1, 0, 384, 512)
+        quantize(0, 1, 0, 256)
+        quantize(0, 1, 256, 512)
+        interleave(vector, 1, 1, 0, 256)
+        interleave(vector, 1, 1, 256, 512)
+        quantize(1, 1, 0, 256)
+        quantize(1, 1, 256, 512)
+
+        def multiply(acc, a, j, h):
+            cols = slice(J_TILE * j, J_TILE * (j + 1))
+            nc.tensor.matmul_mx(
+                out=acc,
+                lhsT=picked[a][:, cols].bitcast(FP8X4),
+                lhsT_scale=picked_scales[SCALE_ROWS * a : P, cols],
+                rhs=w_codes[a][h][:].bitcast(FP8X4),
+                rhs_scale=w_scales[a][h][:],
+                start=(a == 0),
+                stop=(a == PASSES - 1),
+            )
+
+        order = [(j, 0) for j in range(EARLY)]
+        for j in range(EARLY, J_TILES):
+            order += [(j, 0), (j, 1)]
+        order += [(j, 1) for j in range(EARLY)]
+
+        open_banks = {}
+
+        def begin(i):
+            j, h = order[i]
+            acc = psum.tile([P, N_HALF], F32, name="acc")
+            open_banks[i] = acc
+            multiply(acc[:], 0, j, h)
+
+        for i in range(AHEAD):
+            begin(i)
+        for i, (j, h) in enumerate(order):
+            acc = open_banks[i]
+            multiply(acc[:], 1, j, h)
+            cols = slice(N_HALF * h, N_HALF * (h + 1))
+            copy = scalar if i < EARLY or i % 2 == 0 else vector
+            copy(out=results[j][:, cols], in_=acc[:])
+            rows = slice(J_TILE * j, J_TILE * (j + 1))
+            if j < EARLY:
+                nc.sync.dma_start(out=out[rows, cols], in_=results[j][:, cols])
+            elif h == 1:
+                nc.sync.dma_start(out=out[rows, :], in_=results[j][:])
+            if i + AHEAD < len(order):
+                begin(i + AHEAD)

@@ -24,8 +24,8 @@ N_HALF = 512
 J_TILES = S // J_TILE
 SCALE_ROWS = 4
 BANKS = 8
-AHEAD = 4
-EARLY = 6
+AHEAD = 7
+EARLY = 9
 
 
 def tile_list_tabw_tm_none_kernel(tc, tab, w, offs, out):
@@ -40,8 +40,7 @@ def tile_list_tabw_tm_none_kernel(tc, tab, w, offs, out):
         scale_rows = held.tile([P, T // 4], I32, name="scale_rows", align_bytes=64)
         picked = [held.tile([P, S], U32, name=f"picked{a}", align_bytes=64) for a in range(PASSES)]
         picked_scales = held.tile([P, S], U8, name="picked_scales", align_bytes=64)
-        raw0 = held.tile([P, PACK, N], F32, name="raw0")
-        raw1 = [held.tile([P, PACK, N_HALF], F32, name=f"raw1_{h}") for h in range(2)]
+        raw = [[held.tile([P, PACK, N_HALF], F32, name=f"raw{a}_{h}") for h in range(2)] for a in range(PASSES)]
         grouped = [
             [held.tile([P, N_HALF, PACK], BF16, name=f"grouped{a}_{h}", align_bytes=64) for h in range(2)]
             for a in range(PASSES)
@@ -59,32 +58,35 @@ def tile_list_tabw_tm_none_kernel(tc, tab, w, offs, out):
         tab_words = tab.bitcast(I32)
         row_words = T // 4
 
-        nc.sync.dma_start(offsets[:], offs)
-        nc.sync.dma_start(out=words[0][:], in_=tab_words[0, 0 : P * T].rearrange("(p t) -> p t", t=T))
+        def load_w(a, h):
+            nc.sync.dma_start(
+                out=raw[a][h][:],
+                in_=w[K_PASS * a : K_PASS * (a + 1), N_HALF * h : N_HALF * (h + 1)].rearrange("(p i) n -> p i n", i=PACK),
+            )
+
         nc.vector.memset(scale_rows[:], 0)
+        load_w(0, 0)
+        nc.sync.dma_start(offsets[:], offs)
         for q in range(4):
-            nc.scalar.dma_start(
+            nc.sync.dma_start(
                 out=scale_rows[32 * q : 32 * q + PASSES * SCALE_ROWS, :],
                 in_=tab_words[:, P * T : P * T + 16 * row_words].rearrange("a (r t) -> a r t", t=row_words)[
                     :, SCALE_ROWS * q : SCALE_ROWS * (q + 1), :
                 ],
             )
-        nc.sync.dma_start(out=words[1][:], in_=tab_words[1, 0 : P * T].rearrange("(p t) -> p t", t=T))
-        nc.sync.dma_start(out=raw0[:], in_=w[0:K_PASS, :].rearrange("(p i) n -> p i n", i=PACK))
-        for h in range(2):
-            nc.sync.dma_start(
-                out=raw1[h][:],
-                in_=w[K_PASS:K, N_HALF * h : N_HALF * (h + 1)].rearrange("(p i) n -> p i n", i=PACK),
-            )
-
-        nc.vector.tensor_copy(picked_scales[:], scale_rows[:].bitcast(U8).indirect(offsets[:]))
         for a in range(PASSES):
-            nc.vector.tensor_copy(picked[a][:], words[a][:].bitcast(U32).indirect(offsets[:]))
+            nc.sync.dma_start(out=words[a][:], in_=tab_words[a, 0 : P * T].rearrange("(p t) -> p t", t=T))
+            if a == 0:
+                load_w(1, 0)
+        load_w(0, 1)
+        load_w(1, 1)
 
-        def interleave(copy, a, h, c0, c1):
-            src = raw0[:, :, N_HALF * h + c0 : N_HALF * h + c1] if a == 0 else raw1[h][:, :, c0:c1]
+        def interleave(engine, a, h, c0, c1):
+            src = raw[a][h][:, :, c0:c1]
+            dst = grouped[a][h][:, c0:c1, :]
+            copy = nc.vector.tensor_copy if engine == "vector" else nc.scalar.copy
             copy(
-                out=grouped[a][h][:, c0:c1, :].rearrange("p (c i) t -> p c t i", i=4),
+                out=dst.rearrange("p (c i) t -> p c t i", i=4),
                 in_=src.rearrange("p t (c i) -> p c t i", i=4),
             )
 
@@ -95,25 +97,25 @@ def tile_list_tabw_tm_none_kernel(tc, tab, w, offs, out):
                 in_=grouped[a][h][:, c0:c1, :].rearrange("p c t -> p (c t)"),
             )
 
+        nc.vector.tensor_copy(picked_scales[:], scale_rows[:].bitcast(U8).indirect(offsets[:]))
+        interleave("scalar", 0, 0, 0, 256)
+        interleave("scalar", 0, 0, 256, 512)
+        quantize(0, 0, 0, 512)
+        nc.vector.tensor_copy(picked[0][:], words[0][:].bitcast(U32).indirect(offsets[:]))
+        interleave("scalar", 1, 0, 0, 256)
+        interleave("scalar", 1, 0, 256, 512)
+        quantize(1, 0, 0, 512)
+        for b in range(0, S, 512):
+            nc.vector.tensor_copy(
+                picked[1][:, b : b + 512], words[1][:].bitcast(U32).indirect(offsets[:, b // 16 : (b + 512) // 16])
+            )
+        for a in range(PASSES):
+            interleave("vector", a, 1, 0, 256)
+            interleave("vector", a, 1, 256, 512)
+            quantize(a, 1, 0, 256)
+            quantize(a, 1, 256, 512)
+
         vector, scalar = nc.vector.tensor_copy, nc.scalar.copy
-        interleave(vector, 0, 0, 0, 256)
-        interleave(vector, 0, 0, 256, 512)
-        interleave(scalar, 0, 1, 0, 256)
-        interleave(scalar, 0, 1, 256, 512)
-        quantize(0, 0, 0, 256)
-        quantize(0, 0, 256, 512)
-        interleave(scalar, 1, 0, 384, 512)
-        interleave(vector, 1, 0, 0, 256)
-        interleave(vector, 1, 0, 256, 384)
-        quantize(1, 0, 0, 256)
-        quantize(1, 0, 256, 384)
-        quantize(1, 0, 384, 512)
-        quantize(0, 1, 0, 256)
-        quantize(0, 1, 256, 512)
-        interleave(vector, 1, 1, 0, 256)
-        interleave(vector, 1, 1, 256, 512)
-        quantize(1, 1, 0, 256)
-        quantize(1, 1, 256, 512)
 
         def multiply(acc, a, j, h):
             cols = slice(J_TILE * j, J_TILE * (j + 1))

@@ -65,19 +65,26 @@ def tile_list_tabw_tm_none_kernel(tc, tab, w, offs, out):
             )
 
         nc.vector.memset(scale_rows[:], 0)
-        load_w(0, 0)
-        nc.sync.dma_start(offsets[:], offs)
-        for q in range(4):
-            nc.sync.dma_start(
-                out=scale_rows[32 * q : 32 * q + PASSES * SCALE_ROWS, :],
-                in_=tab_words[:, P * T : P * T + 16 * row_words].rearrange("a (r t) -> a r t", t=row_words)[
-                    :, SCALE_ROWS * q : SCALE_ROWS * (q + 1), :
-                ],
-            )
-        for a in range(PASSES):
+
+        def load_words(a):
             nc.sync.dma_start(out=words[a][:], in_=tab_words[a, 0 : P * T].rearrange("(p t) -> p t", t=T))
-            if a == 0:
-                load_w(1, 0)
+
+        def load_scales(r):
+            for a in range(PASSES):
+                nc.sync.dma_start(
+                    out=scale_rows[SCALE_ROWS * a + r : P : 32, :],
+                    in_=tab_words[a, P * T :].rearrange("(r t) -> r t", t=row_words)[r::SCALE_ROWS, :],
+                )
+
+        nc.sync.dma_start(offsets[:], offs)
+        load_scales(0)
+        load_scales(1)
+        load_words(0)
+        load_w(0, 0)
+        load_scales(2)
+        load_scales(3)
+        load_w(1, 0)
+        load_words(1)
         load_w(0, 1)
         load_w(1, 1)
 
@@ -97,18 +104,21 @@ def tile_list_tabw_tm_none_kernel(tc, tab, w, offs, out):
                 in_=grouped[a][h][:, c0:c1, :].rearrange("p c t -> p (c t)"),
             )
 
-        nc.vector.tensor_copy(picked_scales[:], scale_rows[:].bitcast(U8).indirect(offsets[:]))
+        def pick(out_tile, window, b, n):
+            nc.vector.tensor_copy(out_tile[:, b : b + n], window.indirect(offsets[:, b // 16 : (b + n) // 16]))
+
+        for b in range(0, S, 512):
+            pick(picked[0], words[0][:].bitcast(U32), b, 512)
+        pick(picked_scales, scale_rows[:].bitcast(U8), 0, 512)
         interleave("scalar", 0, 0, 0, 256)
         interleave("scalar", 0, 0, 256, 512)
         quantize(0, 0, 0, 512)
-        nc.vector.tensor_copy(picked[0][:], words[0][:].bitcast(U32).indirect(offsets[:]))
+        pick(picked_scales, scale_rows[:].bitcast(U8), 512, 1024)
         interleave("scalar", 1, 0, 0, 256)
         interleave("scalar", 1, 0, 256, 512)
         quantize(1, 0, 0, 512)
         for b in range(0, S, 512):
-            nc.vector.tensor_copy(
-                picked[1][:, b : b + 512], words[1][:].bitcast(U32).indirect(offsets[:, b // 16 : (b + 512) // 16])
-            )
+            pick(picked[1], words[1][:].bitcast(U32), b, 512)
         for a in range(PASSES):
             interleave("vector", a, 1, 0, 256)
             interleave("vector", a, 1, 256, 512)
@@ -129,8 +139,8 @@ def tile_list_tabw_tm_none_kernel(tc, tab, w, offs, out):
                 stop=(a == PASSES - 1),
             )
 
-        order = [(j, 0) for j in range(EARLY)]
-        for j in range(EARLY, J_TILES):
+        order = [(j, 0) for j in range(EARLY + 2)] + [(EARLY, 1), (EARLY + 1, 1)]
+        for j in range(EARLY + 2, J_TILES):
             order += [(j, 0), (j, 1)]
         order += [(j, 1) for j in range(EARLY)]
 
@@ -148,7 +158,7 @@ def tile_list_tabw_tm_none_kernel(tc, tab, w, offs, out):
             acc = open_banks[i]
             multiply(acc[:], 1, j, h)
             cols = slice(N_HALF * h, N_HALF * (h + 1))
-            copy = scalar if i < EARLY or i % 2 == 0 else vector
+            copy = scalar if i < EARLY + 2 or i % 2 == 0 else vector
             copy(out=results[j][:, cols], in_=acc[:])
             rows = slice(J_TILE * j, J_TILE * (j + 1))
             if j < EARLY:

@@ -25,7 +25,7 @@ J_TILES = S // J_TILE
 SCALE_ROWS = 4
 BANKS = 8
 AHEAD = 7
-EARLY = 9
+EARLY = 10
 
 
 def tile_list_tabw_tm_none_kernel(tc, tab, w, offs, out):
@@ -77,9 +77,9 @@ def tile_list_tabw_tm_none_kernel(tc, tab, w, offs, out):
                 )
 
         nc.sync.dma_start(offsets[:], offs)
+        load_words(0)
         load_scales(0)
         load_scales(1)
-        load_words(0)
         load_w(0, 0)
         load_scales(2)
         load_scales(3)
@@ -139,10 +139,7 @@ def tile_list_tabw_tm_none_kernel(tc, tab, w, offs, out):
                 stop=(a == PASSES - 1),
             )
 
-        order = [(j, 0) for j in range(EARLY + 2)] + [(EARLY, 1), (EARLY + 1, 1)]
-        for j in range(EARLY + 2, J_TILES):
-            order += [(j, 0), (j, 1)]
-        order += [(j, 1) for j in range(EARLY)]
+        order = [(j, 0) for j in range(J_TILES)] + [(j, 1) for j in range(EARLY, J_TILES)] + [(j, 1) for j in range(EARLY)]
 
         open_banks = {}
 
@@ -158,7 +155,7 @@ def tile_list_tabw_tm_none_kernel(tc, tab, w, offs, out):
             acc = open_banks[i]
             multiply(acc[:], 1, j, h)
             cols = slice(N_HALF * h, N_HALF * (h + 1))
-            copy = scalar if i < EARLY + 2 or i % 2 == 0 else vector
+            copy = scalar if i < J_TILES or i % 2 == 0 else vector
             copy(out=results[j][:, cols], in_=acc[:])
             rows = slice(J_TILE * j, J_TILE * (j + 1))
             if j < EARLY:

from contextlib import ExitStack

import concourse.mybir as mybir

K, N, T, S = 1024, 1024, 4096, 1536

FLOPS = 2 * K * N * S
BYTES = 2 * 528 * T + 4 * K * N + 2 * 128 * (S // 16) + 4 * S * N

F32 = mybir.dt.float32
BF16 = mybir.dt.bfloat16
I32 = mybir.dt.int32
U32 = mybir.dt.uint32
U16 = mybir.dt.uint16
U8 = mybir.dt.uint8
FP8X4 = mybir.dt.float8_e4m3fn_x4

P = 128
PACK = 4
K_PASS = P * PACK
PASSES = K // K_PASS
J_TILE = 128
N_HALF = 512
J_TILES = S // J_TILE
SCALE_ROWS = 4
BANKS = 8
AHEAD = 7
EARLY = 10


def tile_list_tabw_tm_none_kernel(tc, tab, w, offs, out):
    nc = tc.nc

    with ExitStack() as ctx:
        held = ctx.enter_context(tc.tile_pool(name="held", bufs=1))
        psum = ctx.enter_context(tc.psum_pool(name="psum", bufs=BANKS))

        offsets = held.tile([P, S // 16], U16, name="offsets")
        words = [held.tile([P, T], I32, name=f"words{a}", align_bytes=64) for a in range(PASSES)]
        scale_rows = held.tile([P, T // 4], I32, name="scale_rows", align_bytes=64)
        picked = [held.tile([P, S], U32, name=f"picked{a}", align_bytes=64) for a in range(PASSES)]
        picked_scales = held.tile([P, S], U8, name="picked_scales", align_bytes=64)
        raw = [[held.tile([P, PACK, N_HALF], F32, name=f"raw{a}_{h}") for h in range(2)] for a in range(PASSES)]
        grouped = [
            [held.tile([P, N_HALF, PACK], BF16, name=f"grouped{a}_{h}", align_bytes=64) for h in range(2)]
            for a in range(PASSES)
        ]
        w_codes = [
            [held.tile([P, N_HALF], U32, name=f"w_codes{a}_{h}", align_bytes=64) for h in range(2)]
            for a in range(PASSES)
        ]
        w_scales = [
            [held.tile([P, N_HALF], U8, name=f"w_scales{a}_{h}", align_bytes=64) for h in range(2)]
            for a in range(PASSES)
        ]
        results = [held.tile([P, N], F32, name=f"result{j}") for j in range(J_TILES)]

        tab_words = tab.bitcast(I32)
        row_words = T // 4

        def load_w(a, h):
            nc.sync.dma_start(
                out=raw[a][h][:],
                in_=w[K_PASS * a : K_PASS * (a + 1), N_HALF * h : N_HALF * (h + 1)].rearrange("(p i) n -> p i n", i=PACK),
            )

        nc.vector.memset(scale_rows[:], 0)

        def load_words(a):
            nc.sync.dma_start(out=words[a][:], in_=tab_words[a, 0 : P * T].rearrange("(p t) -> p t", t=T))

        def load_scales(r):
            for a in range(PASSES):
                nc.sync.dma_start(
                    out=scale_rows[SCALE_ROWS * a + r : P : 32, :],
                    in_=tab_words[a, P * T :].rearrange("(r t) -> r t", t=row_words)[r::SCALE_ROWS, :],
                )

        nc.sync.dma_start(offsets[:], offs)
        load_words(0)
        load_scales(0)
        load_scales(1)
        load_w(0, 0)
        load_scales(2)
        load_scales(3)
        load_w(1, 0)
        load_words(1)
        load_w(0, 1)
        load_w(1, 1)

        def interleave(engine, a, h, c0, c1):
            src = raw[a][h][:, :, c0:c1]
            dst = grouped[a][h][:, c0:c1, :]
            copy = nc.vector.tensor_copy if engine == "vector" else nc.scalar.copy
            copy(
                out=dst.rearrange("p (c i) t -> p c t i", i=4),
                in_=src.rearrange("p t (c i) -> p c t i", i=4),
            )

        def quantize(a, h, c0, c1):
            nc.vector.quantize_mx(
                out=w_codes[a][h][:, c0:c1].bitcast(FP8X4),
                scales=w_scales[a][h][:, c0:c1],
                in_=grouped[a][h][:, c0:c1, :].rearrange("p c t -> p (c t)"),
            )

        def pick(out_tile, window, b, n):
            nc.vector.tensor_copy(out_tile[:, b : b + n], window.indirect(offsets[:, b // 16 : (b + n) // 16]))

        for b in range(0, S, 512):
            pick(picked[0], words[0][:].bitcast(U32), b, 512)
        pick(picked_scales, scale_rows[:].bitcast(U8), 0, 512)
        interleave("scalar", 0, 0, 0, 256)
        interleave("scalar", 0, 0, 256, 512)
        quantize(0, 0, 0, 512)
        pick(picked_scales, scale_rows[:].bitcast(U8), 512, 1024)
        interleave("scalar", 1, 0, 0, 256)
        interleave("scalar", 1, 0, 256, 512)
        quantize(1, 0, 0, 512)
        for b in range(0, S, 512):
            pick(picked[1], words[1][:].bitcast(U32), b, 512)
        for a in range(PASSES):
            interleave("vector", a, 1, 0, 256)
            interleave("vector", a, 1, 256, 512)
            quantize(a, 1, 0, 256)
            quantize(a, 1, 256, 512)

        vector, scalar = nc.vector.tensor_copy, nc.scalar.copy

        def multiply(acc, a, j, h):
            cols = slice(J_TILE * j, J_TILE * (j + 1))
            nc.tensor.matmul_mx(
                out=acc,
                lhsT=picked[a][:, cols].bitcast(FP8X4),
                lhsT_scale=picked_scales[SCALE_ROWS * a : P, cols],
                rhs=w_codes[a][h][:].bitcast(FP8X4),
                rhs_scale=w_scales[a][h][:],
                start=(a == 0),
                stop=(a == PASSES - 1),
            )

        order = [(j, 0) for j in range(J_TILES)] + [(j, 1) for j in range(EARLY, J_TILES)] + [(j, 1) for j in range(EARLY)]

        open_banks = {}

        def begin(i):
            j, h = order[i]
            acc = psum.tile([P, N_HALF], F32, name="acc")
            open_banks[i] = acc
            multiply(acc[:], 0, j, h)

        for i in range(AHEAD):
            begin(i)
        for i, (j, h) in enumerate(order):
            acc = open_banks[i]
            multiply(acc[:], 1, j, h)
            cols = slice(N_HALF * h, N_HALF * (h + 1))
            copy = scalar if i < J_TILES or i % 2 == 0 else vector
            copy(out=results[j][:, cols], in_=acc[:])
            rows = slice(J_TILE * j, J_TILE * (j + 1))
            if j < EARLY:
                nc.sync.dma_start(out=out[rows, cols], in_=results[j][:, cols])
            elif h == 1:
                nc.sync.dma_start(out=out[rows, :], in_=results[j][:])
            if i + AHEAD < len(order):
                begin(i + AHEAD)
